import numpy as np
import ml_dtypes


def mxq(x, axis, fmt="e4m3"):
    dtype, down = {"e4m3": (ml_dtypes.float8_e4m3fn, 7), "e5m2": (ml_dtypes.float8_e5m2, 14)}[fmt]
    v = np.moveaxis(np.asarray(x, np.float32).astype(ml_dtypes.bfloat16).astype(np.float64), axis, -1)
    blocks = v.reshape(v.shape[:-1] + (-1, 32))
    amax = np.abs(blocks).max(-1, keepdims=True)
    byte = np.maximum(np.where(amax > 0, np.frexp(amax)[1] - 1 + 127, 0) - down, 1)
    scale = np.exp2(byte - 127.0)
    codes = (blocks / scale).astype(np.float32).astype(dtype).astype(np.float64)
    return np.moveaxis((codes * scale).reshape(v.shape), -1, axis)


WIDE = False


def mx_kscale(k):
    if not WIDE:
        return np.ones(k)
    levels = np.array([10, -10, 5, -5, 0])
    if k % 512:
        return np.exp2(np.random.permutation(np.resize(levels, k // 32))).repeat(32)
    a = np.empty((k // 512, 16))
    for p in range(k // 512):
        a[p, :8] = np.random.permutation(np.resize(levels, 8))
        for g in range(8):
            far = levels[np.abs(levels - a[p, g]) >= 10]
            a[p, g + 8] = far[np.random.randint(len(far))]
    return np.exp2(a.ravel()).repeat(32)


def f64(x):
    return np.asarray(x).astype(np.float64)


def striped8(idx):
    return np.asarray(idx).reshape(8, -1, 16).transpose(0, 2, 1).reshape(128, -1).astype(np.uint16)


def unstriped8(offs):
    return offs.reshape(8, 16, -1).transpose(0, 2, 1).reshape(8, -1).astype(np.int64)


def pick8(x, idx, run):
    r = np.arange(len(x))
    return x[r[:, None], idx[r % (8 * run) // run]]


E2M1 = np.array([0.0, 0.5, 1.0, 1.5, 2.0, 3.0, 4.0, 6.0, -0.0, -0.5, -1.0, -1.5, -2.0, -3.0, -4.0, -6.0])


def pack_weight(w, fmt):
    k, n = w.shape
    w = f64(np.asarray(w, np.float32).astype(ml_dtypes.bfloat16)).reshape(k // 32, 32, n)
    amax = np.abs(w).max(1)
    if fmt == "e4m3":
        byte = np.frexp(amax)[1] - 1 + 127 - 7
    else:
        mant, ex = np.frexp(amax / 6.0)
        byte = np.where(mant > 0.5, ex, ex - 1) + 127
    byte = np.clip(np.where(amax > 0, byte, 1), 1, 254)
    scaled = (w * np.exp2(127.0 - byte)[:, None, :]).reshape(k, n).astype(np.float32)
    by_word = np.ascontiguousarray(scaled.reshape(k // 512, 128, 4, n).transpose(0, 1, 3, 2))
    if fmt == "e4m3":
        words = by_word.astype(ml_dtypes.float8_e4m3fn).view(np.uint8)
    else:
        c = by_word.astype(ml_dtypes.float4_e2m1fn).view(np.uint8) & 0xF
        words = (c[..., 0::2] | (c[..., 1::2] << 4)).reshape(k // 512, 128, 2 * n)
    return np.ascontiguousarray(words), np.ascontiguousarray(byte.astype(np.uint8).reshape(k // 512, 16, n))


def unpack_weight(words, scales, fmt):
    g, _, n = scales.shape
    words = np.ascontiguousarray(words).reshape(g, 128, n, -1)
    if fmt == "e4m3":
        vals = words.view(ml_dtypes.float8_e4m3fn).astype(np.float64)
    else:
        nib = np.empty((g, 128, n, 4), np.uint8)
        nib[..., 0::2] = words & 0xF
        nib[..., 1::2] = words >> 4
        vals = E2M1[nib]
    vals = vals * np.repeat(np.exp2(scales.astype(np.float64) - 127.0), 8, axis=1)[..., None]
    return vals.transpose(0, 1, 3, 2).reshape(g * 512, n)


D, T, I, Q = 512, 1024, 512, 128


def setup_inputs():
    n = np.random.standard_normal
    idx = np.stack([np.random.permutation(T)[:I] for _ in range(8)])
    idx2 = np.stack([np.random.permutation(T)[:I] for _ in range(8)])
    idx3 = np.stack([np.random.permutation(T)[:I] for _ in range(8)])
    idx4 = np.stack([np.random.permutation(T)[:I] for _ in range(8)])
    fd = mx_kscale(D)
    keysp = pack_weight(n((D, T)) / fd[:, None], "e4m3")
    return {
        "query": (n((D, Q)) * 0.9 / np.sqrt(D) * fd[:, None]).astype(np.float32),
        "query2": (n((D, Q)) * 0.9 / np.sqrt(D) * fd[:, None]).astype(np.float32),
        "keys_words": keysp[0],
        "keys_scales": keysp[1],
        "lam": (np.random.uniform(1.0, 2.5, (Q, 1))).astype(np.float32),
        "damp": (np.random.uniform(1.0, 4.0, (Q, 1))).astype(np.float32),
        "old": (np.random.uniform(0.0, 2.0, (Q, T))).astype(np.float32),
        "gainm": (np.random.uniform(0.5, 1.5, (Q, I))).astype(np.float32),
        "offs": striped8(idx),
        "offs2": striped8(idx2),
        "offs3": striped8(idx3),
        "offs4": striped8(idx4),
    }


def reference(query, query2, keys_words, keys_scales, lam, damp, old, gainm, offs, offs2, offs3, offs4):
    idx = unstriped8(offs)
    idx2 = unstriped8(offs2)
    idx3 = unstriped8(offs3)
    idx4 = unstriped8(offs4)
    keysu = unpack_weight(keys_words, keys_scales, "e4m3")
    queryq = mxq(f64(query), 0, "e4m3")
    a = queryq.T @ keysu
    query2q = mxq(f64(query2), 0, "e4m3")
    b = query2q.T @ keysu
    e1s = np.exp(pick8(a, idx, 16))
    s = e1s / (e1s + np.exp(pick8(a, idx2, 16)) + np.exp(pick8(b, idx3, 16))) * f64(lam)
    p = np.exp(s - np.max(s, axis=1, keepdims=True))
    r = p / np.sum(p, axis=1, keepdims=True) * 512.0
    u0 = np.log(r * f64(damp) + 1.0)
    w = u0 / np.sum(u0, axis=1, keepdims=True)
    ws = w * f64(gainm) * 512.0
    wf = np.zeros((Q, T))
    wf[np.arange(Q)[:, None], idx4[np.arange(Q) % 128 // 16]] = ws
    y = f64(old) + wf
    return y

from contextlib import ExitStack

import concourse.mybir as mybir

D, T, I, Q = 512, 1024, 512, 128
FLOPS = 2 * 2 * D * Q * T

F32 = mybir.dt.float32
BF16 = mybir.dt.bfloat16
I32 = mybir.dt.int32
U32 = mybir.dt.uint32
U16 = mybir.dt.uint16
U8 = mybir.dt.uint8
FP8X4 = mybir.dt.float8_e4m3fn_x4
ALU = mybir.AluOpType
ACT = mybir.ActivationFunctionType

P = 128
PACK = 4
HALF_T = T // 2
CH = I // 2
CAP = float(2**30)


def tile_attend_quotaratio_dampened_moved_heads_kernel(
    tc, query, query2, keys_words, keys_scales, lam, damp, old, gainm, offs, offs2, offs3, offs4, out
):
    nc = tc.nc
    with ExitStack() as ctx:
        sb = ctx.enter_context(tc.tile_pool(name="sb", bufs=1))
        ps = ctx.enter_context(tc.psum_pool(name="ps", bufs=1))

        k_scale = sb.tile([P, T], U8, name="k_scale", align_bytes=64)
        nc.vector.memset(k_scale[:].bitcast(I32), 0)
        placed = sb.tile([P, T], F32, name="placed")
        nc.vector.memset(placed[:], 0.0)

        words = keys_words[0].rearrange("p n t -> p (n t)")
        q_raw = [sb.tile([P, PACK, Q], F32, name="q_raw%d" % j) for j in range(2)]
        k_words = [sb.tile([P, HALF_T], U32, name="k_words%d" % h, align_bytes=64) for h in range(2)]

        def load_words(h):
            nc.sync.dma_start(
                out=k_words[h][:].bitcast(I32),
                in_=words[:, h * HALF_T * PACK : (h + 1) * HALF_T * PACK].bitcast(I32),
            )

        nc.sync.dma_start(out=q_raw[0][:], in_=query.rearrange("(p j) m -> p j m", j=PACK))
        load_words(0)
        for g in range(4):
            nc.sync.dma_start(
                out=k_scale[32 * g : 32 * g + 4, :].bitcast(I32),
                in_=keys_scales[0, 4 * g : 4 * g + 4, :].bitcast(I32),
            )
        nc.sync.dma_start(out=q_raw[1][:], in_=query2.rearrange("(p j) m -> p j m", j=PACK))
        load_words(1)

        lists = []
        for j, src in enumerate((offs, offs2, offs3)):
            tile = sb.tile([P, I // 16], U16, name="list%d" % j)
            nc.sync.dma_start(tile[:], src)
            lists.append(tile)
        lam_t = sb.tile([P, 1], F32, name="lam_t")
        nc.sync.dma_start(out=lam_t[:], in_=lam)
        damp_t = sb.tile([P, 1], F32, name="damp_t")
        nc.sync.dma_start(out=damp_t[:], in_=damp)
        gain_t = sb.tile([P, I], F32, name="gain_t")
        nc.sync.dma_start(out=gain_t[:], in_=gainm)
        places = sb.tile([P, I // 16], U16, name="places")
        nc.sync.dma_start(places[:], offs4)
        old_t = sb.tile([P, T], F32, name="old_t")
        nc.sync.dma_start(out=old_t[:], in_=old)

        q_codes, q_scale = [], []
        for j in range(2):
            grouped = sb.tile([P, Q, PACK], BF16, name="grouped%d" % j, align_bytes=64)
            nc.vector.tensor_copy(out=grouped[:], in_=q_raw[j][:].rearrange("p j m -> p m j"))
            codes = sb.tile([P, Q], U32, name="codes%d" % j, align_bytes=64)
            scale = sb.tile([P, Q], U8, name="scale%d" % j, align_bytes=64)
            nc.vector.quantize_mx(
                out=codes[:].bitcast(FP8X4), scales=scale[:], in_=grouped[:].rearrange("p m j -> p (m j)")
            )
            q_codes.append(codes)
            q_scale.append(scale)

        score = [sb.tile([P, T], F32, name="score%d" % j) for j in range(2)]

        def product(j, c0, n, engine):
            bank = ps.tile([P, n], F32, name="bank%d_%d" % (j, c0))
            h, w0 = divmod(c0, HALF_T)
            nc.tensor.matmul_mx(
                out=bank[:],
                lhsT=q_codes[j][:].bitcast(FP8X4),
                lhsT_scale=q_scale[j][:],
                rhs=k_words[h][:, w0 : w0 + n].bitcast(FP8X4),
                rhs_scale=k_scale[:, c0 : c0 + n],
                start=True,
                stop=True,
            )
            if engine == "v":
                nc.vector.tensor_copy(out=score[j][:, c0 : c0 + n], in_=bank[:])
            else:
                nc.scalar.copy(out=score[j][:, c0 : c0 + n], in_=bank[:])

        product(0, 0, 512, "s")
        product(0, 512, 256, "v")
        product(0, 768, 256, "s")

        def entries(j, c):
            return lists[j][:, c * (CH // 16) : (c + 1) * (CH // 16)]

        own = [sb.tile([P, CH], F32, name="own%d" % c) for c in range(2)]
        nc.vector.tensor_copy(own[0][:], score[0][:].indirect(entries(0, 0)))
        nc.scalar.activation(own[1][:], score[0][:].indirect(entries(0, 1)), ACT.Copy)

        product(1, 0, 512, "s")
        product(1, 512, 512, "s")

        half_sign = sb.tile([P, 1], F32, name="half_sign")
        nc.vector.tensor_scalar(half_sign[:], lam_t[:], 0.0, 0.5, ALU.is_ge, ALU.subtract)
        twice_abs = sb.tile([P, 1], F32, name="twice_abs")
        nc.scalar.activation(twice_abs[:], lam_t[:], ACT.Abs, scale=2.0)

        first = []
        for c in range(2):
            gap = sb.tile([P, CH], F32, name="gap_a%d" % c)
            nc.vector.tensor_tensor(gap[:], score[0][:].indirect(entries(1, c)), own[c][:], ALU.subtract)
            ex = sb.tile([P, CH], F32, name="ex_a%d" % c)
            nc.scalar.activation(ex[:], gap[:], ACT.Exp)
            one_plus = sb.tile([P, CH], F32, name="one_plus%d" % c)
            nc.vector.tensor_scalar(one_plus[:], ex[:], CAP, 1.0, ALU.min, ALU.add)
            first.append(one_plus)

        den = []
        for c in range(2):
            gap = sb.tile([P, CH], F32, name="gap_b%d" % c)
            nc.vector.tensor_tensor(gap[:], score[1][:].indirect(entries(2, c)), own[c][:], ALU.subtract)
            ex = sb.tile([P, CH], F32, name="ex_b%d" % c)
            nc.scalar.activation(ex[:], gap[:], ACT.Exp)
            dn = sb.tile([P, CH], F32, name="den%d" % c)
            nc.vector.scalar_tensor_tensor(dn[:], ex[:], CAP, first[c][:], ALU.min, ALU.add)
            den.append(dn)

        H2, H4 = CH // 2, CH // 4
        quad = [sb.tile([P, H4 + c], F32, name="quad%d" % c) for c in range(2)]
        least0 = sb.tile([P, 1], F32, name="least0")
        signed, pair = [], []
        for c in range(2):
            pr = sb.tile([P, H2], F32, name="pair%d" % c)
            nc.vector.tensor_tensor(pr[:], den[c][:, :H2], den[c][:, H2:], ALU.mult)
            pair.append(pr)
            sg = sb.tile([P, CH], F32, name="signed%d" % c)
            if c == 0:
                nc.vector.tensor_scalar(sg[:], den[c][:], half_sign[:], None, ALU.mult, ALU.min, accum_out=least0[:])
            else:
                nc.vector.tensor_scalar(
                    sg[:], den[c][:], half_sign[:], least0[:], ALU.mult, ALU.min, accum_out=quad[1][:, H4 : H4 + 1]
                )
            signed.append(sg)
            nc.vector.tensor_tensor(quad[c][:, :H4], pr[:, :H4], pr[:, H4:], ALU.mult)

        inv_quad = []
        for c in range(2):
            iq = sb.tile([P, H4 + c], F32, name="inv_quad%d" % c)
            nc.vector.reciprocal(iq[:], quad[c][:])
            inv_quad.append(iq)
        neg_max = sb.tile([P, 1], F32, name="neg_max")
        nc.vector.tensor_scalar(neg_max[:], inv_quad[1][:, H4 : H4 + 1], twice_abs[:], -0.25, ALU.mult, ALU.mult)

        prob = sb.tile([P, I], F32, name="prob")
        sums = [sb.tile([P, 1], F32, name="sum%d" % c) for c in range(2)]
        for c in range(2):
            ip = sb.tile([P, 2, H4], F32, name="inv_pair%d" % c)
            nc.vector.tensor_tensor(
                ip[:],
                pair[c][:].rearrange("p (h n) -> p h n", h=2)[:, ::-1, :],
                inv_quad[c][:, :H4].unsqueeze(1).to_broadcast([P, 2, H4]),
                ALU.mult,
            )
            ratio = sb.tile([P, 2, H2], F32, name="ratio%d" % c)
            nc.vector.tensor_tensor(
                ratio[:],
                signed[c][:].rearrange("p (h n) -> p h n", h=2)[:, ::-1, :],
                ip[:].rearrange("p h n -> p (h n)").unsqueeze(1).to_broadcast([P, 2, H2]),
                ALU.mult,
            )
            nc.scalar.activation(
                prob[:, c * CH : (c + 1) * CH],
                ratio[:].rearrange("p h n -> p (h n)"),
                ACT.Exp,
                bias=neg_max[:],
                scale=twice_abs[:],
                accum_out=sums[c][:],
            )

        total = sb.tile([P, 1], F32, name="total")
        nc.vector.tensor_tensor(total[:], sums[0][:], sums[1][:], ALU.add)
        inv_total = sb.tile([P, 1], F32, name="inv_total")
        nc.vector.reciprocal(inv_total[:], total[:])
        factor = sb.tile([P, 1], F32, name="factor")
        nc.vector.tensor_scalar(factor[:], inv_total[:], damp_t[:], float(I), ALU.mult, ALU.mult)

        part = sb.tile([P, I], F32, name="part")
        part_sum = sb.tile([P, 1], F32, name="part_sum")
        nc.scalar.activation(part[:], prob[:], ACT.Ln, bias=1.0, scale=factor[:], accum_out=part_sum[:])
        inv_part = sb.tile([P, 1], F32, name="inv_part")
        nc.vector.reciprocal(inv_part[:], part_sum[:])
        gain_n = sb.tile([P, I], F32, name="gain_n")
        nc.vector.tensor_scalar(gain_n[:], gain_t[:], inv_part[:], float(I), ALU.mult, ALU.mult)

        nc.vector.tensor_tensor(placed[:].indirect(places[:]), part[:], gain_n[:], ALU.mult)

        for h, (c0, c1) in enumerate(((0, 384), (384, 768), (768, 1024))):
            cols = slice(c0, c1)
            res = sb.tile([P, c1 - c0], F32, name="res%d" % h)
            nc.vector.tensor_tensor(res[:], placed[:, cols], old_t[:, cols], ALU.add)
            nc.sync.dma_start(out=out[:, cols], in_=res[:])
